import numpy as np
import ml_dtypes


def mxq(x, axis, fmt="e4m3"):
    dtype, down = {"e4m3": (ml_dtypes.float8_e4m3fn, 7), "e5m2": (ml_dtypes.float8_e5m2, 14)}[fmt]
    v = np.moveaxis(np.asarray(x, np.float32).astype(ml_dtypes.bfloat16).astype(np.float64), axis, -1)
    blocks = v.reshape(v.shape[:-1] + (-1, 32))
    amax = np.abs(blocks).max(-1, keepdims=True)
    byte = np.maximum(np.where(amax > 0, np.frexp(amax)[1] - 1 + 127, 0) - down, 1)
    scale = np.exp2(byte - 127.0)
    codes = (blocks / scale).astype(np.float32).astype(dtype).astype(np.float64)
    return np.moveaxis((codes * scale).reshape(v.shape), -1, axis)


WIDE = False


def mx_kscale(k):
    if not WIDE:
        return np.ones(k)
    levels = np.array([10, -10, 5, -5, 0])
    if k % 512:
        return np.exp2(np.random.permutation(np.resize(levels, k // 32))).repeat(32)
    a = np.empty((k // 512, 16))
    for p in range(k // 512):
        a[p, :8] = np.random.permutation(np.resize(levels, 8))
        for g in range(8):
            far = levels[np.abs(levels - a[p, g]) >= 10]
            a[p, g + 8] = far[np.random.randint(len(far))]
    return np.exp2(a.ravel()).repeat(32)


def f64(x):
    return np.asarray(x).astype(np.float64)


def striped(idx):
    return np.tile(idx.reshape(-1, 16).T, (8, 1)).astype(np.uint16)


def unstriped(offs):
    return offs[:16].T.reshape(-1).astype(np.int64)


E2M1 = np.array([0.0, 0.5, 1.0, 1.5, 2.0, 3.0, 4.0, 6.0, -0.0, -0.5, -1.0, -1.5, -2.0, -3.0, -4.0, -6.0])


def pack_weight(w, fmt):
    k, n = w.shape
    w = f64(np.asarray(w, np.float32).astype(ml_dtypes.bfloat16)).reshape(k // 32, 32, n)
    amax = np.abs(w).max(1)
    if fmt == "e4m3":
        byte = np.frexp(amax)[1] - 1 + 127 - 7
    else:
        mant, ex = np.frexp(amax / 6.0)
        byte = np.where(mant > 0.5, ex, ex - 1) + 127
    byte = np.clip(np.where(amax > 0, byte, 1), 1, 254)
    scaled = (w * np.exp2(127.0 - byte)[:, None, :]).reshape(k, n).astype(np.float32)
    by_word = np.ascontiguousarray(scaled.reshape(k // 512, 128, 4, n).transpose(0, 1, 3, 2))
    if fmt == "e4m3":
        words = by_word.astype(ml_dtypes.float8_e4m3fn).view(np.uint8)
    else:
        c = by_word.astype(ml_dtypes.float4_e2m1fn).view(np.uint8) & 0xF
        words = (c[..., 0::2] | (c[..., 1::2] << 4)).reshape(k // 512, 128, 2 * n)
    return np.ascontiguousarray(words), np.ascontiguousarray(byte.astype(np.uint8).reshape(k // 512, 16, n))


def unpack_weight(words, scales, fmt):
    g, _, n = scales.shape
    words = np.ascontiguousarray(words).reshape(g, 128, n, -1)
    if fmt == "e4m3":
        vals = words.view(ml_dtypes.float8_e4m3fn).astype(np.float64)
    else:
        nib = np.empty((g, 128, n, 4), np.uint8)
        nib[..., 0::2] = words & 0xF
        nib[..., 1::2] = words >> 4
        vals = E2M1[nib]
    vals = vals * np.repeat(np.exp2(scales.astype(np.float64) - 127.0), 8, axis=1)[..., None]
    return vals.transpose(0, 1, 3, 2).reshape(g * 512, n)


def gelu(v):
    return 0.5 * v * (1.0 + np.tanh(np.sqrt(2.0 / np.pi) * (v + 0.044715 * v**3)))


def pack_table4(v):
    words, scales = pack_weight(v, "e2m1")
    g, t = words.shape[0] // 2, v.shape[1]
    words = words.reshape(g, 2, 128, t, 2).transpose(0, 2, 3, 1, 4)
    return np.concatenate([words.reshape(g, -1), scales.reshape(g, -1)], axis=1)


def unpack_table4(tab):
    g, t = tab.shape[0], tab.shape[1] // 544
    words = tab[:, :512 * t].reshape(g, 128, t, 2, 2).transpose(0, 3, 1, 2, 4).reshape(2 * g, 128, 2 * t)
    return unpack_weight(words, tab[:, 512 * t:].reshape(2 * g, 16, t), "e2m1")


K, T, S, H, N = 1024, 4096, 1024, 1536, 256

def setup_inputs():
    n = np.random.standard_normal
    s = mx_kscale(K)[:, None]
    u = mx_kscale(H)[:, None]
    tab = pack_table4(n((K, T)) * s)
    offs = striped(np.random.permutation(T)[:S])
    w1 = (n((K, H)) / np.sqrt(K) / s).astype(np.float32)
    b1 = (0.5 * n(H)).astype(np.float32)
    gain = (np.exp(0.3 * n(H)) * u[:, 0]).astype(np.float32)
    w4_words, w4_scales = pack_weight(1.5 * n((H, N)) / np.sqrt(H) / u, "e2m1")
    lim = np.exp(0.3 * n(N)).astype(np.float32)
    return {"tab": tab, "offs": offs, "w1": w1, "b1": b1, "gain": gain,
            "w4_words": w4_words, "w4_scales": w4_scales, "lim": lim}

def reference(tab, offs, w1, b1, gain, w4_words, w4_scales, lim):
    v = unpack_table4(tab)[:, unstriped(offs)]
    w1q = mxq(f64(w1), 0, "e4m3")
    a = (w1q.T @ v) + f64(b1)[:, None]
    h = f64(gain)[:, None] * np.tanh(a)
    hq = mxq(h, 0, "e4m3")
    w4 = unpack_weight(w4_words, w4_scales, "e2m1")
    y = w4.T @ hq
    return f64(lim)[:, None] * np.tanh(y)

@@ -1,0 +1,181 @@
+from contextlib import ExitStack
+
+import concourse.mybir as mybir
+
+K, T, S, H, N = 1024, 4096, 1024, 1536, 256
+FLOPS = 2 * K * H * S + 2 * H * N * S
+
+F32 = mybir.dt.float32
+BF16 = mybir.dt.bfloat16
+I32 = mybir.dt.int32
+U32 = mybir.dt.uint32
+U16 = mybir.dt.uint16
+U8 = mybir.dt.uint8
+FP8X4 = mybir.dt.float8_e4m3fn_x4
+FP4X4 = mybir.dt.float4_e2m1fn_x4
+TANH = mybir.ActivationFunctionType.Tanh
+MULT = mybir.AluOpType.mult
+
+P = 128
+PACK = 4
+PASS = P * PACK
+COLS = 512
+K_PASSES = K // PASS
+GROUPS = H // PASS
+HALVES = S // COLS
+N_TILES = N // P
+QUADS = 4
+
+
+def tile_list_skill_plan_torques_kernel(tc, tab, offs, w1, b1, gain, w4_words, w4_scales, lim, out):
+    nc = tc.nc
+    with ExitStack() as ctx:
+        held = ctx.enter_context(tc.tile_pool(name="held", bufs=1))
+        ring = ctx.enter_context(tc.tile_pool(name="ring", bufs=3))
+        psum = ctx.enter_context(tc.psum_pool(name="psum", bufs=1))
+
+        offsets = held.tile([P, S // 16], U16, name="offsets")
+        tab_words = held.tile([P, T], I32, name="tab_words", align_bytes=64)
+        tab_scales = held.tile([P, T // 4], I32, name="tab_scales", align_bytes=64)
+        picked_scales = held.tile([P, S], U8, name="picked_scales", align_bytes=64)
+        shifted_scales = held.tile([P, S], U8, name="shifted_scales", align_bytes=64)
+        w4_codes = held.tile([P, GROUPS, 2 * N], U8, name="w4_codes", align_bytes=64)
+        w4_plane = held.tile([P, GROUPS, N], U8, name="w4_plane", align_bytes=64)
+        bias_t = held.tile([P, GROUPS, PACK], F32, name="bias_t")
+        gain_t = held.tile([P, GROUPS, PACK], F32, name="gain_t")
+        lim_t = held.tile([P, N_TILES], F32, name="lim_t")
+        warm = held.tile([P, 2], F32, name="warm")
+
+        w1_raw = {}
+
+        def load_w1(a, g):
+            raw = held.tile([P, PACK, PASS], F32, name="w1_raw_%d_%d" % (a, g), align_bytes=64)
+            rows = w1[g * PASS:(g + 1) * PASS, a * PASS:(a + 1) * PASS]
+            nc.sync.dma_start(out=raw[:], in_=rows.rearrange("(p j) c -> p j c", j=PACK))
+            w1_raw[a, g] = raw
+
+        nc.vector.memset(tab_scales[:], 0)
+        nc.vector.memset(warm[:, 0:1], 0.0)
+        nc.scalar.activation(warm[:, 1:2], warm[:, 0:1], TANH)
+        nc.sync.dma_start(offsets[:], offs)
+        load_w1(0, 0)
+        scale_rows = tab[0, PASS * T:].rearrange("(h q b) -> h q b", h=K_PASSES, q=16).bitcast(I32)
+        for q in range(QUADS):
+            nc.sync.dma_start(out=tab_scales[32 * q:32 * q + 8, :], in_=scale_rows[:, 4 * q:4 * q + 4, :])
+        nc.sync.dma_start(out=tab_words[:], in_=tab[0, 0:PASS * T].rearrange("(p b) -> p b", p=P).bitcast(I32))
+        load_w1(0, 1)
+        for a in range(1, GROUPS):
+            for g in range(K_PASSES):
+                load_w1(a, g)
+            if a == 1:
+                nc.sync.dma_start(out=w4_codes[:].bitcast(I32), in_=w4_words.rearrange("a p b -> p a b").bitcast(I32))
+
+        nc.scalar.dma_start(out=bias_t[:], in_=b1.rearrange("(a p t) -> p a t", p=P, t=PACK))
+        nc.scalar.dma_start(out=gain_t[:], in_=gain.rearrange("(a p t) -> p a t", p=P, t=PACK))
+        nc.gpsimd.memset(shifted_scales[:].bitcast(I32), 0)
+        nc.gpsimd.memset(w4_plane[:].bitcast(I32), 0)
+        for q in range(QUADS):
+            nc.gpsimd.dma_start(
+                out=w4_plane[32 * q:32 * q + 4, :, :].bitcast(I32),
+                in_=w4_scales[:, 4 * q:4 * q + 4, :].rearrange("a r n -> r a n").bitcast(I32))
+        with nc.allow_non_contiguous_dma(reason="one limit a partition"):
+            nc.sync.dma_start(out=lim_t[:], in_=lim.rearrange("(b p) -> p b", p=P))
+
+        w1_codes, w1_plane = {}, {}
+
+        def quantise_w1(a, g, scalar_share):
+            grouped = ring.tile([P, PACK * PASS], BF16, name="w1_grouped", align_bytes=64)
+            dst = grouped[:].rearrange("p (t m j) -> p m j t", t=PACK, j=PACK)
+            src = w1_raw[a, g][:].rearrange("p j (m t) -> p m j t", t=PACK)
+            if scalar_share > 0:
+                nc.scalar.copy(out=dst[:, 0:scalar_share], in_=src[:, 0:scalar_share])
+            if scalar_share < P:
+                nc.vector.tensor_copy(out=dst[:, scalar_share:P], in_=src[:, scalar_share:P])
+            codes = held.tile([P, PASS], U32, name="w1_codes_%d_%d" % (a, g), align_bytes=64)
+            plane = held.tile([P, PASS], U8, name="w1_plane_%d_%d" % (a, g), align_bytes=64)
+            nc.vector.quantize_mx(out=codes[:].bitcast(FP8X4), scales=plane[:], in_=grouped[:])
+            w1_codes[a, g], w1_plane[a, g] = codes, plane
+
+        v_codes = {}
+
+        def pick_words(half):
+            picked = held.tile([P, COLS], U32, name="picked_words_%d" % half, align_bytes=64)
+            entries = offsets[:, half * (COLS // 16):(half + 1) * (COLS // 16)]
+            nc.vector.tensor_copy(picked[:], tab_words[:].bitcast(U32).indirect(entries))
+            parted = held.tile([P, K_PASSES, 2 * COLS], U8, name="v_codes_%d" % half, align_bytes=64)
+            nc.vector.tensor_copy(
+                out=parted[:].bitcast(U16),
+                in_=picked[:].bitcast(U16).rearrange("p (j h) -> p h j", h=K_PASSES))
+            v_codes[half] = parted
+
+        v_plane = (picked_scales, shifted_scales)
+        tanh_tiles = {}
+
+        def first_stage(a, half):
+            cols = slice(half * COLS, (half + 1) * COLS)
+            th = ring.tile([P, PACK, COLS], F32, name="th", align_bytes=64)
+            for t in range(PACK):
+                bank = psum.tile([P, COLS], F32, name="first_bank", bufs=4)
+                m_cols = slice(t * P, (t + 1) * P)
+                for g in range(K_PASSES):
+                    nc.tensor.matmul_mx(
+                        out=bank[:],
+                        lhsT=w1_codes[a, g][:, m_cols].bitcast(FP8X4), lhsT_scale=w1_plane[a, g][:, m_cols],
+                        rhs=v_codes[half][:, g, :].bitcast(FP4X4), rhs_scale=v_plane[g][:, cols],
+                        start=(g == 0), stop=(g == K_PASSES - 1))
+                nc.scalar.activation(th[:, t, :], bank[:], TANH, bias=bias_t[:, a, t:t + 1])
+            tanh_tiles[a, half] = th
+
+        sums = {(half, b): psum.tile([P, COLS], F32, name="sum_%d_%d" % (half, b))
+                for half in range(HALVES) for b in range(N_TILES)}
+
+        def second_stage(a, half):
+            hb = ring.tile([P, PACK * COLS], BF16, name="h_grouped", align_bytes=64)
+            nc.vector.tensor_tensor(
+                hb[:].rearrange("p (c i t) -> p c t i", i=2, t=PACK),
+                tanh_tiles[a, half][:].rearrange("p t (c i) -> p c t i", i=2),
+                gain_t[:, a, :].unsqueeze(1).unsqueeze(3).to_broadcast([P, COLS // 2, PACK, 2]),
+                MULT)
+            codes = ring.tile([P, COLS], U32, name="h_codes", align_bytes=64)
+            plane = ring.tile([P, COLS], U8, name="h_plane", align_bytes=64)
+            nc.vector.quantize_mx(out=codes[:].bitcast(FP8X4), scales=plane[:], in_=hb[:])
+            for b in range(N_TILES):
+                nc.tensor.matmul_mx(
+                    out=sums[half, b][:],
+                    lhsT=w4_codes[:, a, 2 * b * P:2 * (b + 1) * P].bitcast(FP4X4),
+                    lhsT_scale=w4_plane[:, a, b * P:(b + 1) * P],
+                    rhs=codes[:].bitcast(FP8X4), rhs_scale=plane[:],
+                    start=(a == 0), stop=(a == GROUPS - 1))
+
+        def finish(half):
+            for b in range(N_TILES):
+                y = ring.tile([P, COLS], F32, name="y_tanh", align_bytes=64)
+                nc.scalar.activation(y[:], sums[half, b][:], TANH)
+                res = ring.tile([P, COLS], F32, name="result", align_bytes=64)
+                nc.vector.tensor_scalar(res[:], y[:], lim_t[:, b:b + 1], None, MULT)
+                nc.sync.dma_start(out=out[b * P:(b + 1) * P, half * COLS:(half + 1) * COLS], in_=res[:])
+
+        quantise_w1(0, 0, 0)
+        nc.vector.tensor_copy(picked_scales[:], tab_scales[:].bitcast(U8).indirect(offsets[:]))
+        nc.scalar.dma_start(out=shifted_scales[0:P - 4, :].bitcast(I32), in_=picked_scales[4:P, :].bitcast(I32))
+        pick_words(0)
+        quantise_w1(0, 1, 48)
+        pick_words(1)
+        first_stage(0, 0)
+        quantise_w1(1, 0, 0)
+        first_stage(0, 1)
+        second_stage(0, 0)
+        quantise_w1(1, 1, P)
+        first_stage(1, 0)
+        second_stage(0, 1)
+        quantise_w1(2, 0, P)
+        first_stage(1, 1)
+        second_stage(1, 0)
+        quantise_w1(2, 1, P)
+        first_stage(2, 0)
+        second_stage(1, 1)
+        first_stage(2, 1)
+        second_stage(2, 0)
+        finish(0)
+        second_stage(2, 1)
+        finish(1)

@@ -36,76 +36,90 @@ def tile_list_skill_plan_torques_kernel(tc, tab, offs, w1, b1, gain, w4_words, w
 
         offsets = held.tile([P, S // 16], U16, name="offsets")
         tab_words = held.tile([P, T], I32, name="tab_words", align_bytes=64)
-        tab_scales = held.tile([P, T // 4], I32, name="tab_scales", align_bytes=64)
+        tab_scales = held.tile([P, T // 4], I32, name="tab_scales", tag="table", align_bytes=64)
         picked_scales = held.tile([P, S], U8, name="picked_scales", align_bytes=64)
         shifted_scales = held.tile([P, S], U8, name="shifted_scales", align_bytes=64)
-        w4_codes = held.tile([P, GROUPS, 2 * N], U8, name="w4_codes", align_bytes=64)
-        w4_plane = held.tile([P, GROUPS, N], U8, name="w4_plane", align_bytes=64)
         bias_t = held.tile([P, GROUPS, PACK], F32, name="bias_t")
         gain_t = held.tile([P, GROUPS, PACK], F32, name="gain_t")
-        lim_t = held.tile([P, N_TILES], F32, name="lim_t")
+        late_stage = held.tile([P, PACK * PASS], F32, name="late_stage", align_bytes=64)
+        middle = PACK * PASS // 2
+        late_bias = late_stage[:, middle - PACK:middle + PACK].rearrange("p (a t) -> p a t", t=PACK)
         warm = held.tile([P, 2], F32, name="warm")
+
+        banks = [psum.tile([P, COLS], F32, name="bank_%d" % i) for i in range(8)]
 
         w1_raw = {}
 
-        def load_w1(a, g):
-            raw = held.tile([P, PACK, PASS], F32, name="w1_raw_%d_%d" % (a, g), align_bytes=64)
-            rows = w1[g * PASS:(g + 1) * PASS, a * PASS:(a + 1) * PASS]
-            nc.sync.dma_start(out=raw[:], in_=rows.rearrange("(p j) c -> p j c", j=PACK))
-            w1_raw[a, g] = raw
+        def load_w1(a, g, tiles):
+            width = PASS // len(tiles)
+            for piece, raw in enumerate(tiles):
+                first = a * PASS + piece * width
+                rows = w1[g * PASS:(g + 1) * PASS, first:first + width]
+                nc.sync.dma_start(out=raw, in_=rows.rearrange("(p j) c -> p j c", j=PACK))
+            w1_raw[a, g] = tiles
+
+        def raw_tile(tag, width):
+            return held.tile([P, PACK, width], F32, name="w1_raw", tag=tag, align_bytes=64)[:]
 
         nc.vector.memset(tab_scales[:], 0)
         nc.vector.memset(warm[:, 0:1], 0.0)
         nc.scalar.activation(warm[:, 1:2], warm[:, 0:1], TANH)
+        nc.vector.memset(shifted_scales[:].bitcast(I32), 0)
         nc.sync.dma_start(offsets[:], offs)
-        load_w1(0, 0)
+        word_rows = tab[0, 0:PASS * T].rearrange("(p b) -> p b", p=P).bitcast(I32)
         scale_rows = tab[0, PASS * T:].rearrange("(h q b) -> h q b", h=K_PASSES, q=16).bitcast(I32)
+        nc.sync.dma_start(out=tab_words[:, 0:T // 2], in_=word_rows[:, 0:T // 2])
         for q in range(QUADS):
             nc.sync.dma_start(out=tab_scales[32 * q:32 * q + 8, :], in_=scale_rows[:, 4 * q:4 * q + 4, :])
-        nc.sync.dma_start(out=tab_words[:], in_=tab[0, 0:PASS * T].rearrange("(p b) -> p b", p=P).bitcast(I32))
-        load_w1(0, 1)
-        for a in range(1, GROUPS):
-            for g in range(K_PASSES):
-                load_w1(a, g)
-            if a == 1:
-                nc.sync.dma_start(out=w4_codes[:].bitcast(I32), in_=w4_words.rearrange("a p b -> p a b").bitcast(I32))
+        nc.sync.dma_start(out=tab_words[:, T // 2:T], in_=word_rows[:, T // 2:T])
+        for g in range(K_PASSES):
+            load_w1(0, g, [raw_tile("piece_%d_%d" % (g, piece), PASS // 2) for piece in range(2)])
 
-        nc.scalar.dma_start(out=bias_t[:], in_=b1.rearrange("(a p t) -> p a t", p=P, t=PACK))
-        nc.scalar.dma_start(out=gain_t[:], in_=gain.rearrange("(a p t) -> p a t", p=P, t=PACK))
-        nc.gpsimd.memset(shifted_scales[:].bitcast(I32), 0)
-        nc.gpsimd.memset(w4_plane[:].bitcast(I32), 0)
-        for q in range(QUADS):
-            nc.gpsimd.dma_start(
-                out=w4_plane[32 * q:32 * q + 4, :, :].bitcast(I32),
-                in_=w4_scales[:, 4 * q:4 * q + 4, :].rearrange("a r n -> r a n").bitcast(I32))
-        with nc.allow_non_contiguous_dma(reason="one limit a partition"):
-            nc.sync.dma_start(out=lim_t[:], in_=lim.rearrange("(b p) -> p b", p=P))
+        nc.sync.dma_start(out=bias_t[:], in_=b1.rearrange("(a p t) -> p a t", p=P, t=PACK))
+        nc.sync.dma_start(out=gain_t[:], in_=gain.rearrange("(a p t) -> p a t", p=P, t=PACK))
 
-        w1_codes, w1_plane = {}, {}
+        w1_grouped, w1_codes, w1_plane = {}, {}, {}
 
-        def quantise_w1(a, g, scalar_share):
-            grouped = ring.tile([P, PACK * PASS], BF16, name="w1_grouped", align_bytes=64)
-            dst = grouped[:].rearrange("p (t m j) -> p m j t", t=PACK, j=PACK)
-            src = w1_raw[a, g][:].rearrange("p j (m t) -> p m j t", t=PACK)
-            if scalar_share > 0:
-                nc.scalar.copy(out=dst[:, 0:scalar_share], in_=src[:, 0:scalar_share])
-            if scalar_share < P:
-                nc.vector.tensor_copy(out=dst[:, scalar_share:P], in_=src[:, scalar_share:P])
+        def round_w1(a, g, scalar_share):
+            if a == GROUPS - 1:
+                grouped = late_stage[:, g * middle:(g + 1) * middle].bitcast(BF16)
+            elif (a, g) == (1, 1):
+                grouped = tanh_tiles[0, 0].rearrange("p t c -> p (t c)")[:, 0:middle].bitcast(BF16)
+            else:
+                tag = "picked" if a == 1 else "stage_%d" % g
+                grouped = held.tile([P, PACK * PASS], BF16, name="w1_grouped", tag=tag, align_bytes=64)[:]
+            dst = grouped.rearrange("p (t m j) -> p m j t", t=PACK, j=PACK)
+            tiles = w1_raw[a, g]
+            rows = P // len(tiles)
+            for piece, raw in enumerate(tiles):
+                src = raw.rearrange("p j (m t) -> p m j t", t=PACK)
+                m0 = piece * rows
+                cut = min(max(scalar_share - m0, 0), rows)
+                if cut > 0:
+                    nc.scalar.copy(out=dst[:, m0:m0 + cut], in_=src[:, 0:cut])
+                if cut < rows:
+                    nc.vector.tensor_copy(out=dst[:, m0 + cut:m0 + rows], in_=src[:, cut:rows])
+            w1_grouped[a, g] = grouped
+
+        def quantise_w1(a, g, calls):
+            grouped = w1_grouped[a, g]
             codes = held.tile([P, PASS], U32, name="w1_codes_%d_%d" % (a, g), align_bytes=64)
             plane = held.tile([P, PASS], U8, name="w1_plane_%d_%d" % (a, g), align_bytes=64)
-            nc.vector.quantize_mx(out=codes[:].bitcast(FP8X4), scales=plane[:], in_=grouped[:])
+            width = PASS // calls
+            for c in range(calls):
+                cols = slice(c * width, (c + 1) * width)
+                nc.vector.quantize_mx(
+                    out=codes[:, cols].bitcast(FP8X4), scales=plane[:, cols],
+                    in_=grouped[:, PACK * c * width:PACK * (c + 1) * width])
             w1_codes[a, g], w1_plane[a, g] = codes, plane
 
         v_codes = {}
 
-        def pick_words(half):
-            picked = held.tile([P, COLS], U32, name="picked_words_%d" % half, align_bytes=64)
-            entries = offsets[:, half * (COLS // 16):(half + 1) * (COLS // 16)]
-            nc.vector.tensor_copy(picked[:], tab_words[:].bitcast(U32).indirect(entries))
-            parted = held.tile([P, K_PASSES, 2 * COLS], U8, name="v_codes_%d" % half, align_bytes=64)
+        def part_words(picked, half):
+            parted = held.tile([P, K_PASSES, 2 * COLS], U8, name="v_codes", tag="stage_1" if half else "v_codes_0", align_bytes=64)
             nc.vector.tensor_copy(
                 out=parted[:].bitcast(U16),
-                in_=picked[:].bitcast(U16).rearrange("p (j h) -> p h j", h=K_PASSES))
+                in_=picked[:, half * COLS:(half + 1) * COLS].bitcast(U16).rearrange("p (j h) -> p h j", h=K_PASSES))
             v_codes[half] = parted
 
         v_plane = (picked_scales, shifted_scales)
@@ -113,9 +127,13 @@ def tile_list_skill_plan_torques_kernel(tc, tab, offs, w1, b1, gain, w4_words, w
 
         def first_stage(a, half):
             cols = slice(half * COLS, (half + 1) * COLS)
-            th = ring.tile([P, PACK, COLS], F32, name="th", align_bytes=64)
+            if a == 1:
+                th = w1_raw[2, half][0]
+            else:
+                th = held.tile([P, PACK, COLS], F32, name="th", tag="tanh_%d_%d" % (a, half), align_bytes=64)[:]
+            bias = late_bias[:, a, :] if a + half == 1 else bias_t[:, a, :]
             for t in range(PACK):
-                bank = psum.tile([P, COLS], F32, name="first_bank", bufs=4)
+                bank = banks[PACK * half + t]
                 m_cols = slice(t * P, (t + 1) * P)
                 for g in range(K_PASSES):
                     nc.tensor.matmul_mx(
@@ -123,59 +141,123 @@ def tile_list_skill_plan_torques_kernel(tc, tab, offs, w1, b1, gain, w4_words, w
                         lhsT=w1_codes[a, g][:, m_cols].bitcast(FP8X4), lhsT_scale=w1_plane[a, g][:, m_cols],
                         rhs=v_codes[half][:, g, :].bitcast(FP4X4), rhs_scale=v_plane[g][:, cols],
                         start=(g == 0), stop=(g == K_PASSES - 1))
-                nc.scalar.activation(th[:, t, :], bank[:], TANH, bias=bias_t[:, a, t:t + 1])
+                nc.scalar.activation(th[:, t, :], bank[:], TANH, bias=bias[:, t:t + 1])
             tanh_tiles[a, half] = th
 
-        sums = {(half, b): psum.tile([P, COLS], F32, name="sum_%d_%d" % (half, b))
-                for half in range(HALVES) for b in range(N_TILES)}
+        h_grouped, h_codes, h_plane = {}, {}, {}
 
-        def second_stage(a, half):
-            hb = ring.tile([P, PACK * COLS], BF16, name="h_grouped", align_bytes=64)
+        def scale_h(a, half, first, width):
+            if a == 0:
+                hb = w1_grouped[1, half]
+            elif (a, half) == (1, 0):
+                hb = held.tile([P, PACK * width], BF16, name="h_grouped", tag="piece_0_0", align_bytes=64)[:]
+            else:
+                hb = ring.tile([P, PACK * width], BF16, name="h_grouped", align_bytes=64)[:]
             nc.vector.tensor_tensor(
-                hb[:].rearrange("p (c i t) -> p c t i", i=2, t=PACK),
-                tanh_tiles[a, half][:].rearrange("p t (c i) -> p c t i", i=2),
-                gain_t[:, a, :].unsqueeze(1).unsqueeze(3).to_broadcast([P, COLS // 2, PACK, 2]),
+                hb.rearrange("p (c i t) -> p c t i", i=2, t=PACK),
+                tanh_tiles[a, half][:, :, first:first + width].rearrange("p t (c i) -> p c t i", i=2),
+                gain_t[:, a, :].unsqueeze(1).unsqueeze(3).to_broadcast([P, width // 2, PACK, 2]),
                 MULT)
-            codes = ring.tile([P, COLS], U32, name="h_codes", align_bytes=64)
-            plane = ring.tile([P, COLS], U8, name="h_plane", align_bytes=64)
-            nc.vector.quantize_mx(out=codes[:].bitcast(FP8X4), scales=plane[:], in_=hb[:])
-            for b in range(N_TILES):
-                nc.tensor.matmul_mx(
-                    out=sums[half, b][:],
-                    lhsT=w4_codes[:, a, 2 * b * P:2 * (b + 1) * P].bitcast(FP4X4),
-                    lhsT_scale=w4_plane[:, a, b * P:(b + 1) * P],
-                    rhs=codes[:].bitcast(FP8X4), rhs_scale=plane[:],
-                    start=(a == 0), stop=(a == GROUPS - 1))
+            h_grouped[a, half, first] = hb
 
-        def finish(half):
-            for b in range(N_TILES):
-                y = ring.tile([P, COLS], F32, name="y_tanh", align_bytes=64)
-                nc.scalar.activation(y[:], sums[half, b][:], TANH)
-                res = ring.tile([P, COLS], F32, name="result", align_bytes=64)
-                nc.vector.tensor_scalar(res[:], y[:], lim_t[:, b:b + 1], None, MULT)
-                nc.sync.dma_start(out=out[b * P:(b + 1) * P, half * COLS:(half + 1) * COLS], in_=res[:])
+        def quantise_h(a, half, first, width):
+            hb = h_grouped[a, half, first]
+            if first == 0:
+                h_codes[a, half] = ring.tile([P, COLS], U32, name="h_codes", align_bytes=64, bufs=6)
+                h_plane[a, half] = ring.tile([P, COLS], U8, name="h_plane", align_bytes=64, bufs=6)
+            nc.vector.quantize_mx(
+                out=h_codes[a, half][:, first:first + width].bitcast(FP8X4),
+                scales=h_plane[a, half][:, first:first + width], in_=hb)
 
-        quantise_w1(0, 0, 0)
+        spans = [(0, 0, COLS), (1, 0, COLS // 2), (1, COLS // 2, COLS // 2)]
+
+        def sum_banks(half, first, width):
+            if width == COLS:
+                return [(banks[b], [b]) for b in range(N_TILES)]
+            return [(banks[N_TILES + first // width], list(range(N_TILES)))]
+
+        def second_stage(a, half, first, width):
+            step = COLS if width == COLS else P
+            for bank, tiles in sum_banks(half, first, width):
+                for c in range(0, COLS, step):
+                    b = tiles[c // width]
+                    cols = slice(first + c % width, first + c % width + step)
+                    nc.tensor.matmul_mx(
+                        out=bank[:, c:c + step],
+                        lhsT=w4_codes[:, a, 2 * b * P:2 * (b + 1) * P].bitcast(FP4X4),
+                        lhsT_scale=w4_plane[:, a, b * P:(b + 1) * P],
+                        rhs=h_codes[a, half][:, cols].bitcast(FP8X4), rhs_scale=h_plane[a, half][:, cols],
+                        start=(a == 0 and c == 0), stop=(a == GROUPS - 1 and c + step == COLS))
+
+        def finish(half, first, width):
+            col0 = half * COLS + first
+            for bank, tiles in sum_banks(half, first, width):
+                y = ring.tile([P, COLS], F32, name="y_tanh", align_bytes=64, bufs=4)
+                nc.scalar.activation(y[:], bank[:], TANH)
+                res = ring.tile([P, COLS], F32, name="result", align_bytes=64, bufs=4)
+                for i, b in enumerate(tiles):
+                    cols = slice(i * width, (i + 1) * width)
+                    nc.vector.tensor_scalar(res[:, cols], y[:, cols], lim_t[:, b:b + 1], None, MULT)
+                rows = out[tiles[0] * P:(tiles[-1] + 1) * P, col0:col0 + width]
+                nc.sync.dma_start(
+                    out=rows.rearrange("(b p) j -> p b j", p=P),
+                    in_=res[:].rearrange("p (b j) -> p b j", j=width))
+
         nc.vector.tensor_copy(picked_scales[:], tab_scales[:].bitcast(U8).indirect(offsets[:]))
-        nc.scalar.dma_start(out=shifted_scales[0:P - 4, :].bitcast(I32), in_=picked_scales[4:P, :].bitcast(I32))
-        pick_words(0)
-        quantise_w1(0, 1, 48)
-        pick_words(1)
+        nc.sync.dma_start(out=shifted_scales[0:P - 4, :].bitcast(I32), in_=picked_scales[4:P, :].bitcast(I32))
+        chunk = PACK * PASS
+        later = held.tile([P, (GROUPS - 1) * K_PASSES * chunk], F32, name="w1_later", tag="table", align_bytes=64)
+        for i in range((GROUPS - 1) * K_PASSES):
+            rows = later[:, i * chunk:(i + 1) * chunk]
+            load_w1(1 + i // K_PASSES, i % K_PASSES, [rows.rearrange("p (j c) -> p j c", j=PACK)])
+        nc.sync.dma_start(out=late_bias, in_=b1[0:2 * PASS].rearrange("(a p t) -> p a t", p=P, t=PACK))
+        picked_words = held.tile([P, S], U32, name="picked_words", tag="picked", align_bytes=64)
+        nc.vector.tensor_copy(picked_words[:], tab_words[:].bitcast(U32).indirect(offsets[:]))
+        part_words(picked_words, 0)
+        round_w1(0, 0, P)
+        quantise_w1(0, 0, 1)
+        round_w1(0, 1, 96)
+        quantise_w1(0, 1, PACK)
+        part_words(picked_words, 1)
+        round_w1(1, 0, 0)
+        quantise_w1(1, 0, 1)
         first_stage(0, 0)
-        quantise_w1(1, 0, 0)
         first_stage(0, 1)
-        second_stage(0, 0)
-        quantise_w1(1, 1, P)
+        scale_h(0, 0, 0, COLS)
+        round_w1(1, 1, 0)
+        quantise_w1(1, 1, 1)
+        quantise_h(0, 0, 0, COLS)
+        round_w1(2, 0, P)
         first_stage(1, 0)
-        second_stage(0, 1)
-        quantise_w1(2, 0, P)
+        scale_h(0, 1, 0, COLS)
+        quantise_h(0, 1, 0, COLS)
+        quantise_w1(2, 0, 1)
+        round_w1(2, 1, P)
+        scale_h(1, 0, 0, COLS)
+        quantise_w1(2, 1, 1)
+        quantise_h(1, 0, 0, COLS)
+        w4_codes = held.tile([P, GROUPS, 2 * N], U8, name="w4_codes", tag="piece_0_0", align_bytes=64)
+        nc.sync.dma_start(out=w4_codes[:].bitcast(I32), in_=w4_words.rearrange("a p b -> p a b").bitcast(I32))
+        w4_plane = held.tile([P, GROUPS, N], U8, name="w4_plane", tag="tanh_0_1", align_bytes=64)
+        nc.vector.memset(w4_plane[:].bitcast(I32), 0)
+        for q in range(QUADS):
+            nc.sync.dma_start(
+                out=w4_plane[32 * q:32 * q + 4, :, :].bitcast(I32),
+                in_=w4_scales[:, 4 * q:4 * q + 4, :].rearrange("a r n -> r a n").bitcast(I32))
+        lim_t = later[:, 0:N_TILES]
+        with nc.allow_non_contiguous_dma(reason="one limit a partition"):
+            nc.sync.dma_start(out=lim_t, in_=lim.rearrange("(b p) -> p b", p=P))
         first_stage(1, 1)
-        second_stage(1, 0)
-        quantise_w1(2, 1, P)
         first_stage(2, 0)
-        second_stage(1, 1)
+        scale_h(1, 1, 0, COLS)
+        quantise_h(1, 1, 0, COLS)
         first_stage(2, 1)
-        second_stage(2, 0)
-        finish(0)
-        second_stage(2, 1)
-        finish(1)
+        for span in spans:
+            for a in range(GROUPS - 1):
+                second_stage(a, *span)
+        for span in spans:
+            scale_h(GROUPS - 1, *span)
+            quantise_h(GROUPS - 1, *span)
+            second_stage(GROUPS - 1, *span)
+        for span in spans:
+            finish(*span)

@@ -43,7 +43,7 @@ def tile_list_skill_plan_torques_kernel(tc, tab, offs, w1, b1, gain, w4_words, w
         gain_t = held.tile([P, GROUPS, PACK], F32, name="gain_t")
         late_stage = held.tile([P, PACK * PASS], F32, name="late_stage", align_bytes=64)
         middle = PACK * PASS // 2
-        late_bias = late_stage[:, middle - PACK:middle + PACK].rearrange("p (a t) -> p a t", t=PACK)
+        late_bias = late_stage[:, middle - 2:middle + 2]
         warm = held.tile([P, 2], F32, name="warm")
 
         banks = [psum.tile([P, COLS], F32, name="bank_%d" % i) for i in range(8)]
@@ -83,22 +83,20 @@ def tile_list_skill_plan_torques_kernel(tc, tab, offs, w1, b1, gain, w4_words, w
         def round_w1(a, g, scalar_share):
             if a == GROUPS - 1:
                 grouped = late_stage[:, g * middle:(g + 1) * middle].bitcast(BF16)
-            elif (a, g) == (1, 1):
-                grouped = tanh_tiles[0, 0].rearrange("p t c -> p (t c)")[:, 0:middle].bitcast(BF16)
             else:
                 tag = "picked" if a == 1 else "stage_%d" % g
                 grouped = held.tile([P, PACK * PASS], BF16, name="w1_grouped", tag=tag, align_bytes=64)[:]
-            dst = grouped.rearrange("p (t m j) -> p m j t", t=PACK, j=PACK)
+            dst = grouped.rearrange("p (u e m j) -> p u m j e", u=2, e=2, j=PACK)
             tiles = w1_raw[a, g]
             rows = P // len(tiles)
             for piece, raw in enumerate(tiles):
-                src = raw.rearrange("p j (m t) -> p m j t", t=PACK)
+                src = raw.rearrange("p j (m u e) -> p u m j e", u=2, e=2)
                 m0 = piece * rows
                 cut = min(max(scalar_share - m0, 0), rows)
                 if cut > 0:
-                    nc.scalar.copy(out=dst[:, m0:m0 + cut], in_=src[:, 0:cut])
+                    nc.scalar.copy(out=dst[:, :, m0:m0 + cut], in_=src[:, :, 0:cut])
                 if cut < rows:
-                    nc.vector.tensor_copy(out=dst[:, m0 + cut:m0 + rows], in_=src[:, cut:rows])
+                    nc.vector.tensor_copy(out=dst[:, :, m0 + cut:m0 + rows], in_=src[:, :, cut:rows])
             w1_grouped[a, g] = grouped
 
         def quantise_w1(a, g, calls):
@@ -127,11 +125,11 @@ def tile_list_skill_plan_torques_kernel(tc, tab, offs, w1, b1, gain, w4_words, w
 
         def first_stage(a, half):
             cols = slice(half * COLS, (half + 1) * COLS)
-            if a == 1:
-                th = w1_raw[2, half][0]
+            if (a, half) == (1, 1):
+                th = w1_raw[2, 1][0]
             else:
                 th = held.tile([P, PACK, COLS], F32, name="th", tag="tanh_%d_%d" % (a, half), align_bytes=64)[:]
-            bias = late_bias[:, a, :] if a + half == 1 else bias_t[:, a, :]
+            bias = late_bias if (a, half) == (1, 0) else bias_t[:, a, :]
             for t in range(PACK):
                 bank = banks[PACK * half + t]
                 m_cols = slice(t * P, (t + 1) * P)
@@ -147,8 +145,10 @@ def tile_list_skill_plan_torques_kernel(tc, tab, offs, w1, b1, gain, w4_words, w
         h_grouped, h_codes, h_plane = {}, {}, {}
 
         def scale_h(a, half, first, width):
-            if a == 0:
-                hb = w1_grouped[1, half]
+            if (a, half) == (0, 0):
+                hb = w1_grouped[1, 1]
+            elif (a, half) == (0, 1):
+                hb = later[:, chunk:chunk + PACK * width // 2].bitcast(BF16)
             elif (a, half) == (1, 0):
                 hb = held.tile([P, PACK * width], BF16, name="h_grouped", tag="piece_0_0", align_bytes=64)[:]
             else:
@@ -210,7 +210,7 @@ def tile_list_skill_plan_torques_kernel(tc, tab, offs, w1, b1, gain, w4_words, w
         for i in range((GROUPS - 1) * K_PASSES):
             rows = later[:, i * chunk:(i + 1) * chunk]
             load_w1(1 + i // K_PASSES, i % K_PASSES, [rows.rearrange("p (j c) -> p j c", j=PACK)])
-        nc.sync.dma_start(out=late_bias, in_=b1[0:2 * PASS].rearrange("(a p t) -> p a t", p=P, t=PACK))
+        nc.sync.dma_start(out=late_bias, in_=b1[PASS:2 * PASS].rearrange("(p t) -> p t", t=PACK))
         picked_words = held.tile([P, S], U32, name="picked_words", tag="picked", align_bytes=64)
         nc.vector.tensor_copy(picked_words[:], tab_words[:].bitcast(U32).indirect(offsets[:]))
         part_words(picked_words, 0)
@@ -219,26 +219,25 @@ def tile_list_skill_plan_torques_kernel(tc, tab, offs, w1, b1, gain, w4_words, w
         round_w1(0, 1, 96)
         quantise_w1(0, 1, PACK)
         part_words(picked_words, 1)
-        round_w1(1, 0, 0)
-        quantise_w1(1, 0, 1)
+        for g in range(K_PASSES):
+            round_w1(1, g, 0)
+            quantise_w1(1, g, 1)
         first_stage(0, 0)
         first_stage(0, 1)
         scale_h(0, 0, 0, COLS)
-        round_w1(1, 1, 0)
-        quantise_w1(1, 1, 1)
         quantise_h(0, 0, 0, COLS)
-        round_w1(2, 0, P)
         first_stage(1, 0)
         scale_h(0, 1, 0, COLS)
         quantise_h(0, 1, 0, COLS)
+        round_w1(2, 0, P)
         quantise_w1(2, 0, 1)
-        round_w1(2, 1, P)
         scale_h(1, 0, 0, COLS)
+        round_w1(2, 1, 96)
         quantise_w1(2, 1, 1)
         quantise_h(1, 0, 0, COLS)
         w4_codes = held.tile([P, GROUPS, 2 * N], U8, name="w4_codes", tag="piece_0_0", align_bytes=64)
         nc.sync.dma_start(out=w4_codes[:].bitcast(I32), in_=w4_words.rearrange("a p b -> p a b").bitcast(I32))
-        w4_plane = held.tile([P, GROUPS, N], U8, name="w4_plane", tag="tanh_0_1", align_bytes=64)
+        w4_plane = held.tile([P, GROUPS, N], U8, name="w4_plane", tag="picked", align_bytes=64)
         nc.vector.memset(w4_plane[:].bitcast(I32), 0)
         for q in range(QUADS):
             nc.sync.dma_start(

@@ -36,9 +36,7 @@ def tile_list_skill_plan_torques_kernel(tc, tab, offs, w1, b1, gain, w4_words, w
 
         offsets = held.tile([P, S // 16], U16, name="offsets")
         tab_words = held.tile([P, T], I32, name="tab_words", align_bytes=64)
-        tab_scales = held.tile([P, T // 4], I32, name="tab_scales", tag="table", align_bytes=64)
-        picked_scales = held.tile([P, S], U8, name="picked_scales", align_bytes=64)
-        shifted_scales = held.tile([P, S], U8, name="shifted_scales", align_bytes=64)
+        tab_scales = held.tile([P, K_PASSES * T // 4], I32, name="tab_scales", align_bytes=64)
         bias_t = held.tile([P, GROUPS, PACK], F32, name="bias_t")
         gain_t = held.tile([P, GROUPS, PACK], F32, name="gain_t")
         late_stage = held.tile([P, PACK * PASS], F32, name="late_stage", align_bytes=64)
@@ -64,19 +62,27 @@ def tile_list_skill_plan_torques_kernel(tc, tab, offs, w1, b1, gain, w4_words, w
         nc.vector.memset(tab_scales[:], 0)
         nc.vector.memset(warm[:, 0:1], 0.0)
         nc.scalar.activation(warm[:, 1:2], warm[:, 0:1], TANH)
-        nc.vector.memset(shifted_scales[:].bitcast(I32), 0)
         nc.sync.dma_start(offsets[:], offs)
         word_rows = tab[0, 0:PASS * T].rearrange("(p b) -> p b", p=P).bitcast(I32)
-        scale_rows = tab[0, PASS * T:].rearrange("(h q b) -> h q b", h=K_PASSES, q=16).bitcast(I32)
+        scale_rows = tab[0, PASS * T:].rearrange("(h q b) -> q h b", h=K_PASSES, q=16).bitcast(I32)
         nc.sync.dma_start(out=tab_words[:, 0:T // 2], in_=word_rows[:, 0:T // 2])
         for q in range(QUADS):
-            nc.sync.dma_start(out=tab_scales[32 * q:32 * q + 8, :], in_=scale_rows[:, 4 * q:4 * q + 4, :])
+            nc.sync.dma_start(
+                out=tab_scales[32 * q:32 * q + 4, :].rearrange("r (h b) -> r h b", h=K_PASSES),
+                in_=scale_rows[4 * q:4 * q + 4])
         nc.sync.dma_start(out=tab_words[:, T // 2:T], in_=word_rows[:, T // 2:T])
         for g in range(K_PASSES):
             load_w1(0, g, [raw_tile("piece_%d_%d" % (g, piece), PASS // 2) for piece in range(2)])
 
         nc.sync.dma_start(out=bias_t[:], in_=b1.rearrange("(a p t) -> p a t", p=P, t=PACK))
-        nc.sync.dma_start(out=gain_t[:], in_=gain.rearrange("(a p t) -> p a t", p=P, t=PACK))
+        chunk = PACK * PASS
+        later = held.tile([P, (GROUPS - 1) * K_PASSES * chunk], F32, name="w1_later", align_bytes=64)
+        for i in range((GROUPS - 1) * K_PASSES):
+            rows = later[:, i * chunk:(i + 1) * chunk]
+            load_w1(1 + i // K_PASSES, i % K_PASSES, [rows.rearrange("p (j c) -> p j c", j=PACK)])
+            if i == K_PASSES - 1:
+                nc.sync.dma_start(out=gain_t[:], in_=gain.rearrange("(a p t) -> p a t", p=P, t=PACK))
+                nc.sync.dma_start(out=late_bias, in_=b1[PASS:2 * PASS].rearrange("(p t) -> p t", t=PACK))
 
         w1_grouped, w1_codes, w1_plane = {}, {}, {}
 
@@ -120,7 +126,6 @@ def tile_list_skill_plan_torques_kernel(tc, tab, offs, w1, b1, gain, w4_words, w
                 in_=picked[:, half * COLS:(half + 1) * COLS].bitcast(U16).rearrange("p (j h) -> p h j", h=K_PASSES))
             v_codes[half] = parted
 
-        v_plane = (picked_scales, shifted_scales)
         tanh_tiles = {}
 
         def first_stage(a, half):
@@ -203,14 +208,12 @@ def tile_list_skill_plan_torques_kernel(tc, tab, offs, w1, b1, gain, w4_words, w
                     out=rows.rearrange("(b p) j -> p b j", p=P),
                     in_=res[:].rearrange("p (b j) -> p b j", j=width))
 
-        nc.vector.tensor_copy(picked_scales[:], tab_scales[:].bitcast(U8).indirect(offsets[:]))
-        nc.sync.dma_start(out=shifted_scales[0:P - 4, :].bitcast(I32), in_=picked_scales[4:P, :].bitcast(I32))
-        chunk = PACK * PASS
-        later = held.tile([P, (GROUPS - 1) * K_PASSES * chunk], F32, name="w1_later", tag="table", align_bytes=64)
-        for i in range((GROUPS - 1) * K_PASSES):
-            rows = later[:, i * chunk:(i + 1) * chunk]
-            load_w1(1 + i // K_PASSES, i % K_PASSES, [rows.rearrange("p (j c) -> p j c", j=PACK)])
-        nc.sync.dma_start(out=late_bias, in_=b1[PASS:2 * PASS].rearrange("(p t) -> p t", t=PACK))
+        v_plane = []
+        for g in range(K_PASSES):
+            picked_scales = held.tile([P, S], U8, name="picked_scales_%d" % g, align_bytes=64)
+            window = tab_scales[:].bitcast(U8)[:, g * T:(g + 1) * T]
+            nc.vector.tensor_copy(picked_scales[:], window.indirect(offsets[:]))
+            v_plane.append(picked_scales)
         picked_words = held.tile([P, S], U32, name="picked_words", tag="picked", align_bytes=64)
         nc.vector.tensor_copy(picked_words[:], tab_words[:].bitcast(U32).indirect(offsets[:]))
         part_words(picked_words, 0)

@@ -14,17 +14,24 @@ U8 = mybir.dt.uint8
 FP8X4 = mybir.dt.float8_e4m3fn_x4
 FP4X4 = mybir.dt.float4_e2m1fn_x4
 TANH = mybir.ActivationFunctionType.Tanh
+COPY = mybir.ActivationFunctionType.Copy
 MULT = mybir.AluOpType.mult
 
 P = 128
 PACK = 4
 PASS = P * PACK
 COLS = 512
+BANKS = 8
+QUADRANT = 32
+QUADRANTS = P // QUADRANT
+ROWS = 4
 K_PASSES = K // PASS
 GROUPS = H // PASS
-HALVES = S // COLS
 N_TILES = N // P
-QUADS = 4
+CHUNK = PACK * PASS
+ALIGN = 64
+SCALAR_SHARE = 96
+SPANS = [(0, 0, COLS), (1, 0, 2 * P), (1, 2 * P, P), (1, 3 * P, P)]
 
 
 def tile_list_skill_plan_torques_kernel(tc, tab, offs, w1, b1, gain, w4_words, w4_scales, lim, out):
@@ -33,233 +40,245 @@ def tile_list_skill_plan_torques_kernel(tc, tab, offs, w1, b1, gain, w4_words, w
         held = ctx.enter_context(tc.tile_pool(name="held", bufs=1))
         ring = ctx.enter_context(tc.tile_pool(name="ring", bufs=3))
         psum = ctx.enter_context(tc.psum_pool(name="psum", bufs=1))
+        banks = [psum.tile([P, COLS], F32, name="bank_%d" % i) for i in range(BANKS)]
 
         offsets = held.tile([P, S // 16], U16, name="offsets")
-        tab_words = held.tile([P, T], I32, name="tab_words", align_bytes=64)
-        tab_scales = held.tile([P, K_PASSES * T // 4], I32, name="tab_scales", align_bytes=64)
-        bias_t = held.tile([P, GROUPS, PACK], F32, name="bias_t")
-        gain_t = held.tile([P, GROUPS, PACK], F32, name="gain_t")
-        late_stage = held.tile([P, PACK * PASS], F32, name="late_stage", align_bytes=64)
-        middle = PACK * PASS // 2
-        late_bias = late_stage[:, middle - 2:middle + 2]
-        warm = held.tile([P, 2], F32, name="warm")
+        tab_words = held.tile([P, T], I32, name="tab_words", align_bytes=ALIGN)
+        tab_scales = held.tile([P, T // 4], I32, name="tab_scales", tag="scales_then_w1", align_bytes=ALIGN)
+        v_planes = [held.tile([P, S], U8, name="v_plane_%d" % g, align_bytes=ALIGN) for g in range(K_PASSES)]
+        bias_cols = held.tile([P, GROUPS, PACK], F32, name="bias_cols")
 
-        banks = [psum.tile([P, COLS], F32, name="bank_%d" % i) for i in range(8)]
+        nc.vector.memset(tab_scales[:], 0)
+        nc.vector.memset(v_planes[1][:].bitcast(I32), 0)
 
         w1_raw = {}
 
-        def load_w1(a, g, tiles):
-            width = PASS // len(tiles)
-            for piece, raw in enumerate(tiles):
-                first = a * PASS + piece * width
+        def load_w1(a, g, pieces):
+            width = PASS // len(pieces)
+            for i, piece in enumerate(pieces):
+                first = a * PASS + i * width
                 rows = w1[g * PASS:(g + 1) * PASS, first:first + width]
-                nc.sync.dma_start(out=raw, in_=rows.rearrange("(p j) c -> p j c", j=PACK))
-            w1_raw[a, g] = tiles
+                nc.sync.dma_start(out=piece, in_=rows.rearrange("(p j) c -> p j c", j=PACK))
+            w1_raw[a, g] = pieces
 
-        def raw_tile(tag, width):
-            return held.tile([P, PACK, width], F32, name="w1_raw", tag=tag, align_bytes=64)[:]
-
-        nc.vector.memset(tab_scales[:], 0)
-        nc.vector.memset(warm[:, 0:1], 0.0)
-        nc.scalar.activation(warm[:, 1:2], warm[:, 0:1], TANH)
         nc.sync.dma_start(offsets[:], offs)
         word_rows = tab[0, 0:PASS * T].rearrange("(p b) -> p b", p=P).bitcast(I32)
-        scale_rows = tab[0, PASS * T:].rearrange("(h q b) -> q h b", h=K_PASSES, q=16).bitcast(I32)
+        scale_rows = tab[0, PASS * T:].rearrange("(g q b) -> g q b", g=K_PASSES, b=T).bitcast(I32)
         nc.sync.dma_start(out=tab_words[:, 0:T // 2], in_=word_rows[:, 0:T // 2])
-        for q in range(QUADS):
+        nc.sync.dma_start(out=tab_scales[ROWS:P:8, :], in_=scale_rows[1])
+        for quad in range(QUADRANTS):
             nc.sync.dma_start(
-                out=tab_scales[32 * q:32 * q + 4, :].rearrange("r (h b) -> r h b", h=K_PASSES),
-                in_=scale_rows[4 * q:4 * q + 4])
+                out=tab_scales[QUADRANT * quad:QUADRANT * quad + ROWS, :],
+                in_=scale_rows[0, ROWS * quad:ROWS * (quad + 1), :])
         nc.sync.dma_start(out=tab_words[:, T // 2:T], in_=word_rows[:, T // 2:T])
         for g in range(K_PASSES):
-            load_w1(0, g, [raw_tile("piece_%d_%d" % (g, piece), PASS // 2) for piece in range(2)])
+            load_w1(0, g, [
+                held.tile([P, PACK, PASS // 2], F32, name="w1_half", tag="w1_half_%d_%d" % (g, i), align_bytes=ALIGN)[:]
+                for i in range(2)])
+        nc.sync.dma_start(out=bias_cols[:], in_=b1.rearrange("(a p t) -> p a t", p=P, t=PACK))
 
-        nc.sync.dma_start(out=bias_t[:], in_=b1.rearrange("(a p t) -> p a t", p=P, t=PACK))
-        chunk = PACK * PASS
-        later = held.tile([P, (GROUPS - 1) * K_PASSES * chunk], F32, name="w1_later", align_bytes=64)
-        for i in range((GROUPS - 1) * K_PASSES):
-            rows = later[:, i * chunk:(i + 1) * chunk]
-            load_w1(1 + i // K_PASSES, i % K_PASSES, [rows.rearrange("p (j c) -> p j c", j=PACK)])
+        nc.vector.tensor_copy(v_planes[0][:], tab_scales[:].bitcast(U8).indirect(offsets[:]))
+        for r in range(ROWS):
+            nc.sync.dma_start(
+                out=v_planes[1][r:P:QUADRANT, :].bitcast(I32),
+                in_=v_planes[0][8 * r + ROWS:P:QUADRANT, :].bitcast(I32))
+
+        late_chunks = (GROUPS - 1) * K_PASSES
+        late = held.tile([P, (late_chunks + 1) * CHUNK + GROUPS * PACK], F32, name="late", tag="scales_then_w1",
+                         align_bytes=ALIGN)
+        late_raw = [late[:, i * CHUNK:(i + 1) * CHUNK] for i in range(late_chunks)]
+        group_2_stage = late[:, late_chunks * CHUNK:(late_chunks + 1) * CHUNK]
+        gain_cols = late[:, (late_chunks + 1) * CHUNK:].rearrange("p (a t) -> p a t", t=PACK)
+        bias_1_0 = group_2_stage[:, CHUNK // 2 - 2:CHUNK // 2 + 2]
+        for i, raw in enumerate(late_raw):
+            load_w1(1 + i // K_PASSES, i % K_PASSES, [raw.rearrange("p (j c) -> p j c", j=PACK)])
             if i == K_PASSES - 1:
-                nc.sync.dma_start(out=gain_t[:], in_=gain.rearrange("(a p t) -> p a t", p=P, t=PACK))
-                nc.sync.dma_start(out=late_bias, in_=b1[PASS:2 * PASS].rearrange("(p t) -> p t", t=PACK))
-
-        w1_grouped, w1_codes, w1_plane = {}, {}, {}
-
-        def round_w1(a, g, scalar_share):
-            if a == GROUPS - 1:
-                grouped = late_stage[:, g * middle:(g + 1) * middle].bitcast(BF16)
-            else:
-                tag = "picked" if a == 1 else "stage_%d" % g
-                grouped = held.tile([P, PACK * PASS], BF16, name="w1_grouped", tag=tag, align_bytes=64)[:]
-            dst = grouped.rearrange("p (u e m j) -> p u m j e", u=2, e=2, j=PACK)
-            tiles = w1_raw[a, g]
-            rows = P // len(tiles)
-            for piece, raw in enumerate(tiles):
-                src = raw.rearrange("p j (m u e) -> p u m j e", u=2, e=2)
-                m0 = piece * rows
-                cut = min(max(scalar_share - m0, 0), rows)
-                if cut > 0:
-                    nc.scalar.copy(out=dst[:, :, m0:m0 + cut], in_=src[:, :, 0:cut])
-                if cut < rows:
-                    nc.vector.tensor_copy(out=dst[:, :, m0 + cut:m0 + rows], in_=src[:, :, cut:rows])
-            w1_grouped[a, g] = grouped
-
-        def quantise_w1(a, g, calls):
-            grouped = w1_grouped[a, g]
-            codes = held.tile([P, PASS], U32, name="w1_codes_%d_%d" % (a, g), align_bytes=64)
-            plane = held.tile([P, PASS], U8, name="w1_plane_%d_%d" % (a, g), align_bytes=64)
-            width = PASS // calls
-            for c in range(calls):
-                cols = slice(c * width, (c + 1) * width)
-                nc.vector.quantize_mx(
-                    out=codes[:, cols].bitcast(FP8X4), scales=plane[:, cols],
-                    in_=grouped[:, PACK * c * width:PACK * (c + 1) * width])
-            w1_codes[a, g], w1_plane[a, g] = codes, plane
+                nc.sync.dma_start(out=gain_cols, in_=gain.rearrange("(a p t) -> p a t", p=P, t=PACK))
+                nc.sync.dma_start(out=bias_1_0, in_=b1[PASS:2 * PASS].rearrange("(p t) -> p t", t=PACK))
 
         v_codes = {}
 
         def part_words(picked, half):
-            parted = held.tile([P, K_PASSES, 2 * COLS], U8, name="v_codes", tag="stage_1" if half else "v_codes_0", align_bytes=64)
-            nc.vector.tensor_copy(
-                out=parted[:].bitcast(U16),
-                in_=picked[:, half * COLS:(half + 1) * COLS].bitcast(U16).rearrange("p (j h) -> p h j", h=K_PASSES))
+            tag = "w1_0_1_then_v_codes" if half == 1 else "v_codes"
+            parted = held.tile([P, K_PASSES, 2 * COLS], U8, name="v_codes", tag=tag, align_bytes=ALIGN)
+            pairs = picked[:, half * COLS:(half + 1) * COLS].bitcast(U16)
+            nc.vector.tensor_copy(out=parted[:].bitcast(U16), in_=pairs.rearrange("p (j g) -> p g j", g=K_PASSES))
             v_codes[half] = parted
 
-        tanh_tiles = {}
+        w1_rounded, w1_codes, w1_planes = {}, {}, {}
 
-        def first_stage(a, half):
-            cols = slice(half * COLS, (half + 1) * COLS)
-            if (a, half) == (1, 1):
-                th = w1_raw[2, 1][0]
-            else:
-                th = held.tile([P, PACK, COLS], F32, name="th", tag="tanh_%d_%d" % (a, half), align_bytes=64)[:]
-            bias = late_bias if (a, half) == (1, 0) else bias_t[:, a, :]
+        def round_w1(a, g, rounded, scalar_share):
+            dst = rounded.rearrange("p (u e m j) -> p u m j e", u=2, e=2, j=PACK)
+            pieces = w1_raw[a, g]
+            count = P // len(pieces)
+            for i, piece in enumerate(pieces):
+                src = piece.rearrange("p j (m u e) -> p u m j e", u=2, e=2)
+                m0 = i * count
+                cut = min(max(scalar_share - m0, 0), count)
+                if cut > 0:
+                    nc.scalar.copy(out=dst[:, :, m0:m0 + cut], in_=src[:, :, 0:cut])
+                if cut < count:
+                    nc.vector.tensor_copy(out=dst[:, :, m0 + cut:m0 + count], in_=src[:, :, cut:count])
+            w1_rounded[a, g] = rounded
+
+        def quantise_w1(a, g, calls):
+            codes = held.tile([P, PASS], U32, name="w1_codes_%d_%d" % (a, g), align_bytes=ALIGN)
+            plane = held.tile([P, PASS], U8, name="w1_plane_%d_%d" % (a, g), align_bytes=ALIGN)
+            width = PASS // calls
+            for c in range(0, PASS, width):
+                nc.vector.quantize_mx(
+                    out=codes[:, c:c + width].bitcast(FP8X4), scales=plane[:, c:c + width],
+                    in_=w1_rounded[a, g][:, PACK * c:PACK * (c + width)])
+            w1_codes[a, g], w1_planes[a, g] = codes, plane
+
+        def bf16_tile(tag):
+            return held.tile([P, CHUNK], BF16, name="staged", tag=tag, align_bytes=ALIGN)[:]
+
+        def tanh_tile(a, half):
+            return held.tile([P, PACK, COLS], F32, name="tanh_%d_%d" % (a, half), align_bytes=ALIGN)[:]
+
+        tanh_out = {}
+
+        def first_product(a, half, dst, bias):
+            tokens = slice(half * COLS, (half + 1) * COLS)
             for t in range(PACK):
                 bank = banks[PACK * half + t]
                 m_cols = slice(t * P, (t + 1) * P)
                 for g in range(K_PASSES):
                     nc.tensor.matmul_mx(
                         out=bank[:],
-                        lhsT=w1_codes[a, g][:, m_cols].bitcast(FP8X4), lhsT_scale=w1_plane[a, g][:, m_cols],
-                        rhs=v_codes[half][:, g, :].bitcast(FP4X4), rhs_scale=v_plane[g][:, cols],
+                        lhsT=w1_codes[a, g][:, m_cols].bitcast(FP8X4), lhsT_scale=w1_planes[a, g][:, m_cols],
+                        rhs=v_codes[half][:, g, :].bitcast(FP4X4), rhs_scale=v_planes[g][:, tokens],
                         start=(g == 0), stop=(g == K_PASSES - 1))
-                nc.scalar.activation(th[:, t, :], bank[:], TANH, bias=bias[:, t:t + 1])
-            tanh_tiles[a, half] = th
+                nc.scalar.activation(dst[:, t, :], bank[:], TANH, bias=bias[:, t:t + 1])
+            tanh_out[a, half] = dst
 
-        h_grouped, h_codes, h_plane = {}, {}, {}
-
-        def scale_h(a, half, first, width):
-            if (a, half) == (0, 0):
-                hb = w1_grouped[1, 1]
-            elif (a, half) == (0, 1):
-                hb = later[:, chunk:chunk + PACK * width // 2].bitcast(BF16)
-            elif (a, half) == (1, 0):
-                hb = held.tile([P, PACK * width], BF16, name="h_grouped", tag="piece_0_0", align_bytes=64)[:]
-            else:
-                hb = ring.tile([P, PACK * width], BF16, name="h_grouped", align_bytes=64)[:]
+        def gain_on_vector(a, half, dst):
             nc.vector.tensor_tensor(
-                hb.rearrange("p (c i t) -> p c t i", i=2, t=PACK),
-                tanh_tiles[a, half][:, :, first:first + width].rearrange("p t (c i) -> p c t i", i=2),
-                gain_t[:, a, :].unsqueeze(1).unsqueeze(3).to_broadcast([P, width // 2, PACK, 2]),
+                dst.rearrange("p (c i t) -> p c t i", i=2, t=PACK),
+                tanh_out[a, half].rearrange("p t (c i) -> p c t i", i=2),
+                gain_cols[:, a, :].unsqueeze(1).unsqueeze(3).to_broadcast([P, COLS // 2, PACK, 2]),
                 MULT)
-            h_grouped[a, half, first] = hb
 
-        def quantise_h(a, half, first, width):
-            hb = h_grouped[a, half, first]
+        def gain_on_scalar(a, half, first, width, dst):
+            rounded = ring.tile([P, PACK, width], BF16, name="h_rounded", align_bytes=ALIGN)
+            for t in range(PACK):
+                nc.scalar.activation(
+                    rounded[:, t, :], tanh_out[a, half][:, t, first:first + width], COPY,
+                    scale=gain_cols[:, a, t:t + 1])
+            nc.vector.tensor_copy(
+                out=dst.rearrange("p (j t) -> p j t", t=PACK), in_=rounded[:].rearrange("p t j -> p j t"))
+
+        h_codes, h_planes = {}, {}
+
+        def quantise_h(a, half, first, width, interleaved):
             if first == 0:
-                h_codes[a, half] = ring.tile([P, COLS], U32, name="h_codes", align_bytes=64, bufs=6)
-                h_plane[a, half] = ring.tile([P, COLS], U8, name="h_plane", align_bytes=64, bufs=6)
+                h_codes[a, half] = held.tile([P, COLS], U32, name="h_codes_%d_%d" % (a, half), align_bytes=ALIGN)
+                h_planes[a, half] = held.tile([P, COLS], U8, name="h_plane_%d_%d" % (a, half), align_bytes=ALIGN)
             nc.vector.quantize_mx(
                 out=h_codes[a, half][:, first:first + width].bitcast(FP8X4),
-                scales=h_plane[a, half][:, first:first + width], in_=hb)
+                scales=h_planes[a, half][:, first:first + width], in_=interleaved)
 
-        spans = [(0, 0, COLS), (1, 0, COLS // 2), (1, COLS // 2, COLS // 2)]
+        def interleaved_tile(width):
+            return ring.tile([P, PACK * width], BF16, name="h_interleaved", align_bytes=ALIGN)[:]
 
-        def sum_banks(half, first, width):
-            if width == COLS:
+        def sum_banks(span):
+            if span == SPANS[0]:
                 return [(banks[b], [b]) for b in range(N_TILES)]
-            return [(banks[N_TILES + first // width], list(range(N_TILES)))]
+            return [(banks[N_TILES - 1 + SPANS.index(span)], list(range(N_TILES)))]
 
-        def second_stage(a, half, first, width):
+        def second_product(a, span):
+            half, first, width = span
             step = COLS if width == COLS else P
-            for bank, tiles in sum_banks(half, first, width):
-                for c in range(0, COLS, step):
-                    b = tiles[c // width]
-                    cols = slice(first + c % width, first + c % width + step)
+            for bank, n_tiles in sum_banks(span):
+                used = len(n_tiles) * width
+                for c in range(0, used, step):
+                    b = n_tiles[c // width]
+                    tokens = slice(first + c % width, first + c % width + step)
                     nc.tensor.matmul_mx(
                         out=bank[:, c:c + step],
                         lhsT=w4_codes[:, a, 2 * b * P:2 * (b + 1) * P].bitcast(FP4X4),
                         lhsT_scale=w4_plane[:, a, b * P:(b + 1) * P],
-                        rhs=h_codes[a, half][:, cols].bitcast(FP8X4), rhs_scale=h_plane[a, half][:, cols],
-                        start=(a == 0 and c == 0), stop=(a == GROUPS - 1 and c + step == COLS))
+                        rhs=h_codes[a, half][:, tokens].bitcast(FP8X4), rhs_scale=h_planes[a, half][:, tokens],
+                        start=(a == 0 and c == 0), stop=(a == GROUPS - 1 and c + step == used))
 
-        def finish(half, first, width):
-            col0 = half * COLS + first
-            for bank, tiles in sum_banks(half, first, width):
-                y = ring.tile([P, COLS], F32, name="y_tanh", align_bytes=64, bufs=4)
-                nc.scalar.activation(y[:], bank[:], TANH)
-                res = ring.tile([P, COLS], F32, name="result", align_bytes=64, bufs=4)
-                for i, b in enumerate(tiles):
+        def finish(span):
+            half, first, width = span
+            token = half * COLS + first
+            for bank, n_tiles in sum_banks(span):
+                used = len(n_tiles) * width
+                squashed = held.tile([P, used], F32, name="squashed_%d_%d" % (token, n_tiles[0]), align_bytes=ALIGN)
+                nc.scalar.activation(squashed[:], bank[:, 0:used], TANH)
+                result = held.tile([P, used], F32, name="result_%d_%d" % (token, n_tiles[0]), align_bytes=ALIGN)
+                for i, b in enumerate(n_tiles):
                     cols = slice(i * width, (i + 1) * width)
-                    nc.vector.tensor_scalar(res[:, cols], y[:, cols], lim_t[:, b:b + 1], None, MULT)
-                rows = out[tiles[0] * P:(tiles[-1] + 1) * P, col0:col0 + width]
+                    nc.vector.tensor_scalar(result[:, cols], squashed[:, cols], lim_cols[:, b:b + 1], None, MULT)
+                rows = out[n_tiles[0] * P:(n_tiles[-1] + 1) * P, token:token + width]
                 nc.sync.dma_start(
                     out=rows.rearrange("(b p) j -> p b j", p=P),
-                    in_=res[:].rearrange("p (b j) -> p b j", j=width))
+                    in_=result[:].rearrange("p (b j) -> p b j", j=width))
 
-        v_plane = []
-        for g in range(K_PASSES):
-            picked_scales = held.tile([P, S], U8, name="picked_scales_%d" % g, align_bytes=64)
-            window = tab_scales[:].bitcast(U8)[:, g * T:(g + 1) * T]
-            nc.vector.tensor_copy(picked_scales[:], window.indirect(offsets[:]))
-            v_plane.append(picked_scales)
-        picked_words = held.tile([P, S], U32, name="picked_words", tag="picked", align_bytes=64)
+        picked_words = held.tile([P, S], U32, name="picked_words", tag="vector_chain", align_bytes=ALIGN)
         nc.vector.tensor_copy(picked_words[:], tab_words[:].bitcast(U32).indirect(offsets[:]))
         part_words(picked_words, 0)
-        round_w1(0, 0, P)
+        round_w1(0, 0, bf16_tile("w1_0_0"), P)
         quantise_w1(0, 0, 1)
-        round_w1(0, 1, 96)
+        round_w1(0, 1, bf16_tile("w1_0_1_then_v_codes"), SCALAR_SHARE)
         quantise_w1(0, 1, PACK)
         part_words(picked_words, 1)
+
         for g in range(K_PASSES):
-            round_w1(1, g, 0)
+            round_w1(1, g, bf16_tile("vector_chain"), 0)
             quantise_w1(1, g, 1)
-        first_stage(0, 0)
-        first_stage(0, 1)
-        scale_h(0, 0, 0, COLS)
-        quantise_h(0, 0, 0, COLS)
-        first_stage(1, 0)
-        scale_h(0, 1, 0, COLS)
-        quantise_h(0, 1, 0, COLS)
-        round_w1(2, 0, P)
+        for half in range(2):
+            first_product(0, half, tanh_tile(0, half), bias_cols[:, 0, :])
+        h_0_0 = w1_rounded[1, 1]
+        gain_on_vector(0, 0, h_0_0)
+        quantise_h(0, 0, 0, COLS, h_0_0)
+        first_product(1, 0, tanh_tile(1, 0), bias_1_0)
+        h_0_1 = late_raw[1][:, 0:CHUNK // 2].bitcast(BF16)
+        gain_on_vector(0, 1, h_0_1)
+        quantise_h(0, 1, 0, COLS, h_0_1)
+
+        round_w1(2, 0, group_2_stage[:, 0:CHUNK // 2].bitcast(BF16), P)
         quantise_w1(2, 0, 1)
-        scale_h(1, 0, 0, COLS)
-        round_w1(2, 1, 96)
+        h_1_0 = bf16_tile("w1_half_0_0")
+        gain_on_vector(1, 0, h_1_0)
+        round_w1(2, 1, group_2_stage[:, CHUNK // 2:CHUNK].bitcast(BF16), SCALAR_SHARE)
         quantise_w1(2, 1, 1)
-        quantise_h(1, 0, 0, COLS)
-        w4_codes = held.tile([P, GROUPS, 2 * N], U8, name="w4_codes", tag="piece_0_0", align_bytes=64)
+        quantise_h(1, 0, 0, COLS, h_1_0)
+
+        w4_codes = held.tile([P, GROUPS, 2 * N], U8, name="w4_codes", tag="w1_half_0_0", align_bytes=ALIGN)
         nc.sync.dma_start(out=w4_codes[:].bitcast(I32), in_=w4_words.rearrange("a p b -> p a b").bitcast(I32))
-        w4_plane = held.tile([P, GROUPS, N], U8, name="w4_plane", tag="picked", align_bytes=64)
+        w4_plane = held.tile([P, GROUPS, N], U8, name="w4_plane", tag="vector_chain", align_bytes=ALIGN)
         nc.vector.memset(w4_plane[:].bitcast(I32), 0)
-        for q in range(QUADS):
+        for quad in range(QUADRANTS):
             nc.sync.dma_start(
-                out=w4_plane[32 * q:32 * q + 4, :, :].bitcast(I32),
-                in_=w4_scales[:, 4 * q:4 * q + 4, :].rearrange("a r n -> r a n").bitcast(I32))
-        lim_t = later[:, 0:N_TILES]
-        with nc.allow_non_contiguous_dma(reason="one limit a partition"):
-            nc.sync.dma_start(out=lim_t, in_=lim.rearrange("(b p) -> p b", p=P))
-        first_stage(1, 1)
-        first_stage(2, 0)
-        scale_h(1, 1, 0, COLS)
-        quantise_h(1, 1, 0, COLS)
-        first_stage(2, 1)
-        for span in spans:
-            for a in range(GROUPS - 1):
-                second_stage(a, *span)
-        for span in spans:
-            scale_h(GROUPS - 1, *span)
-            quantise_h(GROUPS - 1, *span)
-            second_stage(GROUPS - 1, *span)
-        for span in spans:
-            finish(*span)
+                out=w4_plane[QUADRANT * quad:QUADRANT * quad + ROWS, :, :].bitcast(I32),
+                in_=w4_scales[:, ROWS * quad:ROWS * (quad + 1), :].rearrange("a r n -> r a n").bitcast(I32))
+        lim_cols = late_raw[0][:, 0:N_TILES]
+        with nc.allow_non_contiguous_dma(reason="one limit for each partition and tile of output rows"):
+            nc.sync.dma_start(out=lim_cols, in_=lim.rearrange("(b p) -> p b", p=P))
+
+        first_product(1, 1, w1_raw[2, 1][0], bias_cols[:, 1, :])
+        first_product(2, 0, tanh_tile(2, 0), bias_cols[:, 2, :])
+        h_1_1 = interleaved_tile(COLS)
+        gain_on_vector(1, 1, h_1_1)
+        quantise_h(1, 1, 0, COLS, h_1_1)
+        first_product(2, 1, tanh_tile(2, 1), bias_cols[:, 2, :])
+
+        last = GROUPS - 1
+        for span in SPANS:
+            for a in range(last):
+                second_product(a, span)
+        for span in SPANS:
+            half, first, width = span
+            interleaved = interleaved_tile(width)
+            if half == 0:
+                gain_on_vector(last, half, interleaved)
+            else:
+                gain_on_scalar(last, half, first, width, interleaved)
+            quantise_h(last, half, first, width, interleaved)
+            second_product(last, span)
+        for span in SPANS:
+            finish(span)

from contextlib import ExitStack

import concourse.mybir as mybir

K, T, S, H, N = 1024, 4096, 1024, 1536, 256
FLOPS = 2 * K * H * S + 2 * H * N * S

F32 = mybir.dt.float32
BF16 = mybir.dt.bfloat16
I32 = mybir.dt.int32
U32 = mybir.dt.uint32
U16 = mybir.dt.uint16
U8 = mybir.dt.uint8
FP8X4 = mybir.dt.float8_e4m3fn_x4
FP4X4 = mybir.dt.float4_e2m1fn_x4
TANH = mybir.ActivationFunctionType.Tanh
COPY = mybir.ActivationFunctionType.Copy
MULT = mybir.AluOpType.mult

P = 128
PACK = 4
PASS = P * PACK
COLS = 512
BANKS = 8
QUADRANT = 32
QUADRANTS = P // QUADRANT
ROWS = 4
K_PASSES = K // PASS
GROUPS = H // PASS
N_TILES = N // P
CHUNK = PACK * PASS
ALIGN = 64
SCALAR_SHARE = 96
SPANS = [(0, 0, COLS), (1, 0, 2 * P), (1, 2 * P, P), (1, 3 * P, P)]


def tile_list_skill_plan_torques_kernel(tc, tab, offs, w1, b1, gain, w4_words, w4_scales, lim, out):
    nc = tc.nc
    with ExitStack() as ctx:
        held = ctx.enter_context(tc.tile_pool(name="held", bufs=1))
        ring = ctx.enter_context(tc.tile_pool(name="ring", bufs=3))
        psum = ctx.enter_context(tc.psum_pool(name="psum", bufs=1))
        banks = [psum.tile([P, COLS], F32, name="bank_%d" % i) for i in range(BANKS)]

        offsets = held.tile([P, S // 16], U16, name="offsets")
        tab_words = held.tile([P, T], I32, name="tab_words", align_bytes=ALIGN)
        tab_scales = held.tile([P, T // 4], I32, name="tab_scales", tag="scales_then_w1", align_bytes=ALIGN)
        v_planes = [held.tile([P, S], U8, name="v_plane_%d" % g, align_bytes=ALIGN) for g in range(K_PASSES)]
        bias_cols = held.tile([P, GROUPS, PACK], F32, name="bias_cols")

        nc.vector.memset(tab_scales[:], 0)
        nc.vector.memset(v_planes[1][:].bitcast(I32), 0)

        w1_raw = {}

        def load_w1(a, g, pieces):
            width = PASS // len(pieces)
            for i, piece in enumerate(pieces):
                first = a * PASS + i * width
                rows = w1[g * PASS:(g + 1) * PASS, first:first + width]
                nc.sync.dma_start(out=piece, in_=rows.rearrange("(p j) c -> p j c", j=PACK))
            w1_raw[a, g] = pieces

        nc.sync.dma_start(offsets[:], offs)
        word_rows = tab[0, 0:PASS * T].rearrange("(p b) -> p b", p=P).bitcast(I32)
        scale_rows = tab[0, PASS * T:].rearrange("(g q b) -> g q b", g=K_PASSES, b=T).bitcast(I32)
        nc.sync.dma_start(out=tab_words[:, 0:T // 2], in_=word_rows[:, 0:T // 2])
        nc.sync.dma_start(out=tab_scales[ROWS:P:8, :], in_=scale_rows[1])
        for quad in range(QUADRANTS):
            nc.sync.dma_start(
                out=tab_scales[QUADRANT * quad:QUADRANT * quad + ROWS, :],
                in_=scale_rows[0, ROWS * quad:ROWS * (quad + 1), :])
        nc.sync.dma_start(out=tab_words[:, T // 2:T], in_=word_rows[:, T // 2:T])
        for g in range(K_PASSES):
            load_w1(0, g, [
                held.tile([P, PACK, PASS // 2], F32, name="w1_half", tag="w1_half_%d_%d" % (g, i), align_bytes=ALIGN)[:]
                for i in range(2)])
        nc.sync.dma_start(out=bias_cols[:], in_=b1.rearrange("(a p t) -> p a t", p=P, t=PACK))

        nc.vector.tensor_copy(v_planes[0][:], tab_scales[:].bitcast(U8).indirect(offsets[:]))
        for r in range(ROWS):
            nc.sync.dma_start(
                out=v_planes[1][r:P:QUADRANT, :].bitcast(I32),
                in_=v_planes[0][8 * r + ROWS:P:QUADRANT, :].bitcast(I32))

        late_chunks = (GROUPS - 1) * K_PASSES
        late = held.tile([P, (late_chunks + 1) * CHUNK + GROUPS * PACK], F32, name="late", tag="scales_then_w1",
                         align_bytes=ALIGN)
        late_raw = [late[:, i * CHUNK:(i + 1) * CHUNK] for i in range(late_chunks)]
        group_2_stage = late[:, late_chunks * CHUNK:(late_chunks + 1) * CHUNK]
        gain_cols = late[:, (late_chunks + 1) * CHUNK:].rearrange("p (a t) -> p a t", t=PACK)
        bias_1_0 = group_2_stage[:, CHUNK // 2 - 2:CHUNK // 2 + 2]
        for i, raw in enumerate(late_raw):
            load_w1(1 + i // K_PASSES, i % K_PASSES, [raw.rearrange("p (j c) -> p j c", j=PACK)])
            if i == K_PASSES - 1:
                nc.sync.dma_start(out=gain_cols, in_=gain.rearrange("(a p t) -> p a t", p=P, t=PACK))
                nc.sync.dma_start(out=bias_1_0, in_=b1[PASS:2 * PASS].rearrange("(p t) -> p t", t=PACK))

        v_codes = {}

        def part_words(picked, half):
            tag = "w1_0_1_then_v_codes" if half == 1 else "v_codes"
            parted = held.tile([P, K_PASSES, 2 * COLS], U8, name="v_codes", tag=tag, align_bytes=ALIGN)
            pairs = picked[:, half * COLS:(half + 1) * COLS].bitcast(U16)
            nc.vector.tensor_copy(out=parted[:].bitcast(U16), in_=pairs.rearrange("p (j g) -> p g j", g=K_PASSES))
            v_codes[half] = parted

        w1_rounded, w1_codes, w1_planes = {}, {}, {}

        def round_w1(a, g, rounded, scalar_share):
            dst = rounded.rearrange("p (u e m j) -> p u m j e", u=2, e=2, j=PACK)
            pieces = w1_raw[a, g]
            count = P // len(pieces)
            for i, piece in enumerate(pieces):
                src = piece.rearrange("p j (m u e) -> p u m j e", u=2, e=2)
                m0 = i * count
                cut = min(max(scalar_share - m0, 0), count)
                if cut > 0:
                    nc.scalar.copy(out=dst[:, :, m0:m0 + cut], in_=src[:, :, 0:cut])
                if cut < count:
                    nc.vector.tensor_copy(out=dst[:, :, m0 + cut:m0 + count], in_=src[:, :, cut:count])
            w1_rounded[a, g] = rounded

        def quantise_w1(a, g, calls):
            codes = held.tile([P, PASS], U32, name="w1_codes_%d_%d" % (a, g), align_bytes=ALIGN)
            plane = held.tile([P, PASS], U8, name="w1_plane_%d_%d" % (a, g), align_bytes=ALIGN)
            width = PASS // calls
            for c in range(0, PASS, width):
                nc.vector.quantize_mx(
                    out=codes[:, c:c + width].bitcast(FP8X4), scales=plane[:, c:c + width],
                    in_=w1_rounded[a, g][:, PACK * c:PACK * (c + width)])
            w1_codes[a, g], w1_planes[a, g] = codes, plane

        def bf16_tile(tag):
            return held.tile([P, CHUNK], BF16, name="staged", tag=tag, align_bytes=ALIGN)[:]

        def tanh_tile(a, half):
            return held.tile([P, PACK, COLS], F32, name="tanh_%d_%d" % (a, half), align_bytes=ALIGN)[:]

        tanh_out = {}

        def first_product(a, half, dst, bias):
            tokens = slice(half * COLS, (half + 1) * COLS)
            for t in range(PACK):
                bank = banks[PACK * half + t]
                m_cols = slice(t * P, (t + 1) * P)
                for g in range(K_PASSES):
                    nc.tensor.matmul_mx(
                        out=bank[:],
                        lhsT=w1_codes[a, g][:, m_cols].bitcast(FP8X4), lhsT_scale=w1_planes[a, g][:, m_cols],
                        rhs=v_codes[half][:, g, :].bitcast(FP4X4), rhs_scale=v_planes[g][:, tokens],
                        start=(g == 0), stop=(g == K_PASSES - 1))
                nc.scalar.activation(dst[:, t, :], bank[:], TANH, bias=bias[:, t:t + 1])
            tanh_out[a, half] = dst

        def gain_on_vector(a, half, dst):
            nc.vector.tensor_tensor(
                dst.rearrange("p (c i t) -> p c t i", i=2, t=PACK),
                tanh_out[a, half].rearrange("p t (c i) -> p c t i", i=2),
                gain_cols[:, a, :].unsqueeze(1).unsqueeze(3).to_broadcast([P, COLS // 2, PACK, 2]),
                MULT)

        def gain_on_scalar(a, half, first, width, dst):
            rounded = ring.tile([P, PACK, width], BF16, name="h_rounded", align_bytes=ALIGN)
            for t in range(PACK):
                nc.scalar.activation(
                    rounded[:, t, :], tanh_out[a, half][:, t, first:first + width], COPY,
                    scale=gain_cols[:, a, t:t + 1])
            nc.vector.tensor_copy(
                out=dst.rearrange("p (j t) -> p j t", t=PACK), in_=rounded[:].rearrange("p t j -> p j t"))

        h_codes, h_planes = {}, {}

        def quantise_h(a, half, first, width, interleaved):
            if first == 0:
                h_codes[a, half] = held.tile([P, COLS], U32, name="h_codes_%d_%d" % (a, half), align_bytes=ALIGN)
                h_planes[a, half] = held.tile([P, COLS], U8, name="h_plane_%d_%d" % (a, half), align_bytes=ALIGN)
            nc.vector.quantize_mx(
                out=h_codes[a, half][:, first:first + width].bitcast(FP8X4),
                scales=h_planes[a, half][:, first:first + width], in_=interleaved)

        def interleaved_tile(width):
            return ring.tile([P, PACK * width], BF16, name="h_interleaved", align_bytes=ALIGN)[:]

        def sum_banks(span):
            if span == SPANS[0]:
                return [(banks[b], [b]) for b in range(N_TILES)]
            return [(banks[N_TILES - 1 + SPANS.index(span)], list(range(N_TILES)))]

        def second_product(a, span):
            half, first, width = span
            step = COLS if width == COLS else P
            for bank, n_tiles in sum_banks(span):
                used = len(n_tiles) * width
                for c in range(0, used, step):
                    b = n_tiles[c // width]
                    tokens = slice(first + c % width, first + c % width + step)
                    nc.tensor.matmul_mx(
                        out=bank[:, c:c + step],
                        lhsT=w4_codes[:, a, 2 * b * P:2 * (b + 1) * P].bitcast(FP4X4),
                        lhsT_scale=w4_plane[:, a, b * P:(b + 1) * P],
                        rhs=h_codes[a, half][:, tokens].bitcast(FP8X4), rhs_scale=h_planes[a, half][:, tokens],
                        start=(a == 0 and c == 0), stop=(a == GROUPS - 1 and c + step == used))

        def finish(span):
            half, first, width = span
            token = half * COLS + first
            for bank, n_tiles in sum_banks(span):
                used = len(n_tiles) * width
                squashed = held.tile([P, used], F32, name="squashed_%d_%d" % (token, n_tiles[0]), align_bytes=ALIGN)
                nc.scalar.activation(squashed[:], bank[:, 0:used], TANH)
                result = held.tile([P, used], F32, name="result_%d_%d" % (token, n_tiles[0]), align_bytes=ALIGN)
                for i, b in enumerate(n_tiles):
                    cols = slice(i * width, (i + 1) * width)
                    nc.vector.tensor_scalar(result[:, cols], squashed[:, cols], lim_cols[:, b:b + 1], None, MULT)
                rows = out[n_tiles[0] * P:(n_tiles[-1] + 1) * P, token:token + width]
                nc.sync.dma_start(
                    out=rows.rearrange("(b p) j -> p b j", p=P),
                    in_=result[:].rearrange("p (b j) -> p b j", j=width))

        picked_words = held.tile([P, S], U32, name="picked_words", tag="vector_chain", align_bytes=ALIGN)
        nc.vector.tensor_copy(picked_words[:], tab_words[:].bitcast(U32).indirect(offsets[:]))
        part_words(picked_words, 0)
        round_w1(0, 0, bf16_tile("w1_0_0"), P)
        quantise_w1(0, 0, 1)
        round_w1(0, 1, bf16_tile("w1_0_1_then_v_codes"), SCALAR_SHARE)
        quantise_w1(0, 1, PACK)
        part_words(picked_words, 1)

        for g in range(K_PASSES):
            round_w1(1, g, bf16_tile("vector_chain"), 0)
            quantise_w1(1, g, 1)
        for half in range(2):
            first_product(0, half, tanh_tile(0, half), bias_cols[:, 0, :])
        h_0_0 = w1_rounded[1, 1]
        gain_on_vector(0, 0, h_0_0)
        quantise_h(0, 0, 0, COLS, h_0_0)
        first_product(1, 0, tanh_tile(1, 0), bias_1_0)
        h_0_1 = late_raw[1][:, 0:CHUNK // 2].bitcast(BF16)
        gain_on_vector(0, 1, h_0_1)
        quantise_h(0, 1, 0, COLS, h_0_1)

        round_w1(2, 0, group_2_stage[:, 0:CHUNK // 2].bitcast(BF16), P)
        quantise_w1(2, 0, 1)
        h_1_0 = bf16_tile("w1_half_0_0")
        gain_on_vector(1, 0, h_1_0)
        round_w1(2, 1, group_2_stage[:, CHUNK // 2:CHUNK].bitcast(BF16), SCALAR_SHARE)
        quantise_w1(2, 1, 1)
        quantise_h(1, 0, 0, COLS, h_1_0)

        w4_codes = held.tile([P, GROUPS, 2 * N], U8, name="w4_codes", tag="w1_half_0_0", align_bytes=ALIGN)
        nc.sync.dma_start(out=w4_codes[:].bitcast(I32), in_=w4_words.rearrange("a p b -> p a b").bitcast(I32))
        w4_plane = held.tile([P, GROUPS, N], U8, name="w4_plane", tag="vector_chain", align_bytes=ALIGN)
        nc.vector.memset(w4_plane[:].bitcast(I32), 0)
        for quad in range(QUADRANTS):
            nc.sync.dma_start(
                out=w4_plane[QUADRANT * quad:QUADRANT * quad + ROWS, :, :].bitcast(I32),
                in_=w4_scales[:, ROWS * quad:ROWS * (quad + 1), :].rearrange("a r n -> r a n").bitcast(I32))
        lim_cols = late_raw[0][:, 0:N_TILES]
        with nc.allow_non_contiguous_dma(reason="one limit for each partition and tile of output rows"):
            nc.sync.dma_start(out=lim_cols, in_=lim.rearrange("(b p) -> p b", p=P))

        first_product(1, 1, w1_raw[2, 1][0], bias_cols[:, 1, :])
        first_product(2, 0, tanh_tile(2, 0), bias_cols[:, 2, :])
        h_1_1 = interleaved_tile(COLS)
        gain_on_vector(1, 1, h_1_1)
        quantise_h(1, 1, 0, COLS, h_1_1)
        first_product(2, 1, tanh_tile(2, 1), bias_cols[:, 2, :])

        last = GROUPS - 1
        for span in SPANS:
            for a in range(last):
                second_product(a, span)
        for span in SPANS:
            half, first, width = span
            interleaved = interleaved_tile(width)
            if half == 0:
                gain_on_vector(last, half, interleaved)
            else:
                gain_on_scalar(last, half, first, width, interleaved)
            quantise_h(last, half, first, width, interleaved)
            second_product(last, span)
        for span in SPANS:
            finish(span)
